import numpy as np, ml_dtypes
CORES = [88,96,104,112,120,216,224,232,240,248]
N = 10
import mx_ref
NC, G = 512, 4
C = np.float32(2.0 ** -5)
CNT = [[16,0,48,192,80,0,96,80,0,0],[96,80,0,0,96,176,0,48,0,16],[32,80,0,0,96,0,112,0,16,176],[0,0,96,0,0,80,176,80,64,16],[96,128,0,80,16,16,0,160,16,0],[0,80,96,32,112,96,0,0,0,96],[16,0,96,96,32,16,80,16,0,160],[160,0,16,96,80,80,16,16,0,48],[96,96,160,16,0,0,32,96,16,0],[0,48,0,0,0,48,0,16,400,0]]
OFF = [[sum(c[:e]) for e in range(N + 1)] for c in CNT]
BF = ml_dtypes.bfloat16
def cut(t, i, w=512):
    return t[:, w * i:w * i + w]
def tile(rs):
    return np.stack(rs, axis=2).reshape(128, -1).astype(BF)
def layer(w, X):
    out = []
    for i in range(G):
        for t in range(len(X)):
            p = mx_ref.matmul(mx_ref.quantize(cut(w, len(X) * i + t)), X[t])
            z = p if t == 0 else z + p
        out.append(z)
    return out
def gated(Z, g):
    return [(np.maximum(z, 0) * C) * g for z in Z]
def setup_inputs(rng):
    def f(*shape):
        return mx_ref.flush((rng.standard_normal(shape, dtype=np.float32) * np.exp2(rng.integers(-2, 3, shape[:-1] + (1,)))).astype(BF))
    gt = np.broadcast_to((0.125 + 0.875 * rng.random((N, 1, NC))).astype(BF), (N, 128, NC)).copy()
    return {"gt": gt, "x": f(N, 128, 4 * NC), "w1": f(N, 128, G * 512), "w2": f(N, 128, 512)}
def setup_inputs_blocks(rng):
    d = setup_inputs(rng)
    for k in ("x", "w1", "w2"): d[k] = mx_ref.spread(d[k], rng, 4)
    return d
def setup_inputs_wide(rng):
    d = setup_inputs(rng)
    for k in ("x", "w1", "w2"): d[k] = mx_ref.flush((d[k].astype(np.float32) * np.exp2(rng.integers(-8, 9, (N, 1, 1))).astype(np.float32)).astype(BF))
    return d
def setup_inputs_zeros(rng):
    d = setup_inputs(rng); v = d["x"].reshape(N, 128, -1, 4).copy()
    v[np.broadcast_to((rng.random((N, 1, v.shape[2], 1)) < 0.33), v.shape)] = 0
    d["x"] = v.reshape(d["x"].shape)
    return d
def reference(gt, x, w1, w2):
    y = np.zeros((N, 128, NC), np.float32)
    for e in range(N):
        t = np.concatenate([x[j][:, 4 * OFF[j][e]:4 * OFF[j][e + 1]] for j in range(N)], axis=1)
        g = np.concatenate([gt[j][:, OFF[j][e]:OFF[j][e + 1]] for j in range(N)], axis=1).astype(np.float32)
        y[e] = mx_ref.matmul(mx_ref.quantize(w2[e]), mx_ref.quantize(tile(gated(layer(w1[e], [mx_ref.quantize(t)]), g))))
    return {"y": y}

@@ -1,0 +1,357 @@
+from concourse.bass import DstId, RemoteDMATransfer
+from concourse.mybir import dt, AluOpType, ActivationFunctionType
+
+NC, G, EDGE, NCH = 512, 4, 128, 3
+CORES_SIMULATED = 256
+C = 2.0 ** -5
+
+HELP = [
+    [[[(6, 0, 96)]], [[(2, 0, 48)]], [[(3, 0, 96)]], [[(3, 96, 96)]]],
+    [[[(0, 0, 96)]], [[(4, 0, 96)]], [[(5, 0, 128)]], [[(5, 128, 48), (7, 0, 48)], [(9, 0, 16)]]],
+    [[[(1, 0, 80)]], [[(8, 0, 16)]], [[(6, 0, 112)]], [[(4, 0, 96)]]],
+    [[[(5, 0, 80)]], [[(9, 0, 16)]], [[(2, 0, 96)]], [[(7, 0, 80)]]],
+    [[[(3, 0, 80)]], [[(8, 0, 16)]], [[(1, 0, 128)]], [[(0, 0, 96)]]],
+    [[[(1, 0, 80)]], [[(3, 0, 32)]], [[(4, 0, 64)]], [[(4, 64, 48)]]],
+    [[[(4, 0, 32)], [(5, 0, 16)]], [[(9, 0, 48)], [(7, 0, 16)]], [[(2, 0, 96)], [(0, 0, 16)]], [[(9, 48, 112)]]],
+    [[[(3, 0, 96)]], [[(0, 0, 80)]], [[(9, 0, 48)], [(6, 0, 16)]], [[(0, 80, 80)]]],
+    [[[(0, 0, 96)]], [[(2, 0, 80)]], [[(7, 0, 96)]], [[(2, 80, 80)], [(3, 0, 16)]]],
+    [[[(8, 144, 128)]], [[(8, 272, 128)]], [[(1, 0, 48)]], [[(8, 0, 144)]]],
+]
+DIRECT = [[[4, 7]], [], [[9], [0]], [[6], [8]], [[7], [5]], [[2, 9]], [[3]], [[4, 5], [2]], [[1], [6]], [[5], [7]]]
+
+SCRATCH = {
+    "xb": ("sbuf", [128, 4 * NC], "bfloat16"),
+    "w1b": ("sbuf", [128, 4 * NC], "bfloat16"),
+    "w2b": ("sbuf", [128, NC], "bfloat16"),
+    "xq": ("sbuf", [128, NC], "float8_e4m3fn_x4"),
+    "xs": ("sbuf", [128, NC], "uint8"),
+    "w1q": ("sbuf", [128, NC], "float8_e4m3fn_x4"),
+    "w1s": ("sbuf", [128, NC], "uint8"),
+    "w2q": ("sbuf", [128, 128], "float8_e4m3fn_x4"),
+    "w2s": ("sbuf", [128, 128], "uint8"),
+    "hc": ("sbuf", [128, 192], "float8_e4m3fn_x4"),
+    "hp": ("sbuf", [128, 192], "uint8"),
+    "bc": ("sbuf", [128, NC + 2 * EDGE], "float8_e4m3fn_x4"),
+    "bs": ("sbuf", [128, NC + 2 * EDGE], "uint8"),
+    "gd": ("dram", [128, 4], "bfloat16"),
+    "gl": ("dram", [10, 128, 4], "bfloat16"),
+    "grow": ("sbuf", [128, NC], "bfloat16"),
+    "gb": ("sbuf", [128, NC], "bfloat16"),
+    "hb": ("sbuf", [128, 4 * NC], "bfloat16"),
+    "hq": ("sbuf", [128, NC], "float8_e4m3fn_x4"),
+    "hs": ("sbuf", [128, NC], "uint8"),
+    "ysb": ("sbuf", [128, NC], "float32"),
+    "ps": ("psum", [128, 8 * NC], "float32"),
+}
+SEMAPHORES = (["gtl", "xl0", "xl1", "wl1", "wl2", "xqd", "own", "wq1", "wq2", "go", "ls", "hgs", "hcs", "hps",
+               "mm", "my", "vm", "vr", "sr", "hqd", "yst"]
+              + ["g%d" % j for j in range(10)] + ["ch%d" % c for c in range(NCH)]
+              + ["gth%d" % c for c in range(NCH)] + ["gbd%d" % c for c in range(NCH)] + ["yc%d" % c for c in range(NCH)])
+
+
+def bits(mask):
+    return [b for b in range(mask.bit_length()) if mask >> b & 1]
+
+
+def share(mask, k, n):
+    return sum(1 << b for b in bits(mask)[k::n])
+
+
+def make_plan(tables):
+    cnt, n = tables["CNT"], len(tables["CNT"])
+    off = [[sum(row[:e]) for e in range(n + 1)] for row in cnt]
+    pieces = [[] for _ in range(n)]
+    first = {}
+    for j in range(n):
+        if cnt[j][j]:
+            pieces[j].append((-1, j, 0, cnt[j][j]))
+        for k, calls in enumerate(HELP[j]):
+            for i, call in enumerate(calls):
+                for e, s, m in call:
+                    pieces[e].append((10 + i, j, s, m))
+                    first.setdefault((j, e), k)
+        for i, call in enumerate(DIRECT[j]):
+            for e in call:
+                pieces[e].append((i, j, 0, cnt[j][e]))
+                first[(j, e)] = -1
+    place, chunks, turned = {}, [], []
+    for e in range(n):
+        pieces[e].sort()
+        turn = bool(cnt[e][e]) and off[e][e + 1] < 128
+        turned.append(turn)
+        at, ends = 0, []
+        for _, j, s, m in pieces[e]:
+            place[(e, j, s)] = NC - at - m if turn else at
+            at += m
+            ends.append(at)
+        best = None
+        for a in range(128, 257, 16):
+            for b in range(a + 128, NC - 127, 16):
+                v = abs(a - 240) / 16 + abs(b - 384) / 16 + (0 if a in ends else 3) + (0 if b in ends else 3)
+                if best is None or v < best[0]:
+                    best = (v, a, b)
+        cut = [0, best[1], best[2], NC]
+        chunks.append([(NC - cut[c + 1], NC - cut[c]) if turn else (cut[c], cut[c + 1]) for c in range(NCH)])
+    base = [[sum(cnt[i][e] for i in range(j)) for j in range(n)] for e in range(n)]
+
+    def chunk_of(e, p, m):
+        return min(c for c in range(NCH) if p < chunks[e][c][1] and p + m > chunks[e][c][0])
+    return {"cnt": cnt, "off": off, "pieces": pieces, "first": first, "place": place, "chunks": chunks,
+            "turned": turned, "base": base, "chunk_of": chunk_of}
+
+
+def windows(P, j):
+    spans = []
+    for calls in HELP[j]:
+        cols = [(P["off"][j][e] + s, P["off"][j][e] + s + m) for call in calls for e, s, m in call]
+        spans.append((min(a for a, _ in cols), max(b for _, b in cols)))
+    w = max(b - a for a, b in spans)
+    return w, [min(a, NC - w) for a, _ in spans]
+
+
+def rank_program(g, core, T, topo):
+    cores = T.cores
+    rank = T.rank_of(core)
+    known = {}
+
+    def same_chip(a, b):
+        return topo.chip(a) == topo.chip(b) and topo.host(a) == topo.host(b)
+
+    def helpers(j):
+        if j not in known:
+            r = cores[j]
+            own = [c for c in range(CORES_SIMULATED)
+                   if c != r and same_chip(c, r) and all(topo.may_write(c, d) for d in cores)]
+            known[j] = sorted(own, key=lambda c: (topo.die(c) != topo.die(r), c))
+        return known[j]
+
+    serves = [j for j in range(len(cores)) if same_chip(core, cores[j]) and (rank is not None or core in helpers(j))]
+    if not serves:
+        return
+    P = make_plan(T.tables)
+    sent = [0]
+
+    def dst(d):
+        rid, pid = topo.addr(d, core)
+        return DstId(rid=rid, pnc=pid)
+
+    def send(parts):
+        sent[0] += sum(len(bits(p[4])) for p in parts)
+        if len(parts) == 1:
+            src, d, out, sem, mask = parts[0]
+            rid, pid = topo.addr(d, core)
+            g.remote_dma(out, src, sem, T.sem.ls, pid, rid, mask)
+        else:
+            g.remote_dma_fused([RemoteDMATransfer(dst_ids=[dst(d)], dma_engine_mask=mask, remote_sem=sem, src=src, dst=out)
+                                for src, d, out, sem, mask in parts], local_sem=T.sem.ls)
+
+    def send_gates(outs, sem, mask):
+        sent[0] += len(bits(mask))
+        g.remote_dma_fused([RemoteDMATransfer(dst_ids=[dst(d) for d, _ in outs], dma_engine_mask=mask, remote_sem=sem,
+                                              srcs=[T.gd[:]], dsts=[o for _, o in outs])], local_sem=T.sem.ls)
+
+    def codes(t, a, b):
+        return t[:, a:b].bitcast(dt.uint8)
+
+    def pass_on(j, call, qc, qs, first_col, before):
+        for kind in range(2):
+            before(kind)
+            parts = []
+            for i, (e, s, m) in enumerate(call):
+                a = P["off"][j][e] + s - first_col
+                p = P["place"][(e, j, s)]
+                sem = T.sem["ch%d" % P["chunk_of"](e, p, m)]
+                mask = share(topo.mask(core, cores[e]), i, len(call))
+                if kind == 0:
+                    parts.append((codes(qc, a, a + m), cores[e], codes(T.bc, EDGE + p, EDGE + p + m), sem, mask))
+                else:
+                    parts.append((qs[:, a:a + m], cores[e], T.bs[:, EDGE + p:EDGE + p + m], sem, mask))
+            send(parts)
+
+    if rank is None:
+        j = serves[0]
+        k = helpers(j).index(core)
+        starts = windows(P, j)[1]
+        here = len(bits(topo.mask(cores[j], core)))
+        to = sorted(e for (src, e), by in P["first"].items() if src == j and by == k)
+        g.wait_ge(T.sem.hgs, here)
+        if to:
+            send_gates([(cores[e], T.gl[j]) for e in to], T.sem["g%d" % j], topo.mask(core, cores[to[0]]))
+        for call in HELP[j][k]:
+            pass_on(j, call, T.hc, T.hp, starts[k],
+                    lambda kind: g.wait_ge([T.sem.hcs, T.sem.hps][kind], here // 4))
+        g.wait_ge(T.sem.ls, sent[0])
+        return
+
+    cnt, off = P["cnt"], P["off"]
+    hs = helpers(rank)
+    width, starts = windows(P, rank)
+    chunks = P["chunks"][rank]
+    own = cnt[rank][rank]
+    where = sorted((P["place"][(rank, j, s)], j, s, m) for _, j, s, m in P["pieces"][rank])
+    sy, sc, v, te = g.sync, g.scalar, g.vector, g.tensor
+
+    sy.dma_start(T.gd[:], T.gt[0:1, :]).then_inc(T.sem.gtl, 16)
+    sc.dma_start(T.xb[:, 0:2 * NC], T.x[:, 0:2 * NC]).then_inc(T.sem.xl0, 16)
+    sy.dma_start(T.xb[:, 2 * NC:4 * NC], T.x[:, 2 * NC:4 * NC]).then_inc(T.sem.xl1, 16)
+
+    runs = [[] for _ in range(NCH)]
+    for p, j, s, m in where:
+        r = runs[P["chunk_of"](rank, p, m)]
+        t0 = off[j][rank] + s
+        if r and r[-1][1] == j and r[-1][0] + r[-1][3] == p and r[-1][2] + r[-1][3] == t0:
+            r[-1] = (r[-1][0], j, r[-1][2], r[-1][3] + m)
+        else:
+            r.append((p, j, t0, m))
+    for c in range(NCH):
+        for p, j, t0, m in runs[c]:
+            if j == rank:
+                sy.dma_start(T.grow[0:1, p:p + m], T.gt[0:1, t0:t0 + m]).then_inc(T.sem["gth%d" % c], 16)
+
+    sy.wait_ge(T.sem.go, 1)
+    sy.dma_start(T.w1b[:], T.w1[:]).then_inc(T.sem.wl1, 16)
+    sy.dma_start(T.w2b[:], T.w2[:]).then_inc(T.sem.wl2, 16)
+
+    seen = set()
+    for c in range(NCH):
+        todo = [r for r in runs[c] if r[1] != rank]
+        todo.sort(key=lambda r: (P["first"][(r[1], rank)] >= 0, r[1]))
+        for p, j, t0, m in todo:
+            if j not in seen:
+                seen.add(j)
+                sender = P["first"][(j, rank)]
+                src = cores[j] if sender < 0 else helpers(j)[sender]
+                sy.wait_ge(T.sem["g%d" % j], len(bits(topo.mask(src, core))))
+            sy.dma_start(T.grow[0:1, p:p + m], T.gl[j, t0 // 4:(t0 + m) // 4, :]).then_inc(T.sem["gth%d" % c], 16)
+
+    near = topo.mask(core, hs[0])
+    g.wait_ge(T.sem.gtl, 16)
+    send_gates([(h, T.gd[:]) for h in hs], T.sem.hgs, near)
+    straight = [cores[e] for call in DIRECT[rank] for e in call]
+    if straight:
+        send_gates([(d, T.gl[rank]) for d in straight], T.sem["g%d" % rank], topo.mask(core, straight[0]))
+    g.wait_ge(T.sem.xqd, 2)
+    turn = [0, 2, 1, 3]
+    send([(codes(T.xq, a, a + width), h, codes(T.hc, 0, width), T.sem.hcs, share(near, turn[k], 4))
+          for k, (h, a) in enumerate(zip(hs, starts))])
+    send([(T.xs[:, a:a + width], h, T.hp[:, 0:width], T.sem.hps, share(near, turn[k], 4))
+          for k, (h, a) in enumerate(zip(hs, starts))])
+    g.sem_inc(T.sem.go, 1)
+    for call in DIRECT[rank]:
+        pass_on(rank, [(e, 0, cnt[rank][e]) for e in call], T.xq, T.xs, 0, lambda kind: None)
+    for c in range(NCH):
+        a, b = chunks[c]
+        if runs[c]:
+            g.wait_ge(T.sem["gth%d" % c], 16 * len(runs[c]))
+        g.partition_broadcast(T.gb[:, a:b], T.grow[0:1, a:b], 128).then_inc(T.sem["gbd%d" % c], 1)
+    g.wait_ge(T.sem.ls, sent[0])
+
+    v.wait_ge(T.sem.xl0, 16)
+    v.quantize_mx(T.xq[:, 0:NC // 2], T.xs[:, 0:NC // 2], T.xb[:, 0:2 * NC]).then_inc(T.sem.xqd, 1)
+    v.wait_ge(T.sem.xl1, 16)
+    v.quantize_mx(T.xq[:, NC // 2:NC], T.xs[:, NC // 2:NC], T.xb[:, 2 * NC:4 * NC]).then_inc(T.sem.xqd, 1)
+    if own:
+        if P["turned"][rank]:
+            xa, ba = off[rank][rank], EDGE + NC - own
+        else:
+            xa, ba = off[rank][rank + 1] - 128, EDGE + own - 128
+        v.quantize_mx(T.bc[:, ba:ba + 128], T.bs[:, ba:ba + 128], T.xb[:, 4 * xa:4 * (xa + 128)]).then_inc(T.sem.own, 1)
+    v.wait_ge(T.sem.wl1, 16)
+    v.quantize_mx(T.w1q[:], T.w1s[:], T.w1b[:]).then_inc(T.sem.wq1, 1)
+    v.wait_ge(T.sem.wl2, 16)
+    v.quantize_mx(T.w2q[:], T.w2s[:], T.w2b[:]).then_inc(T.sem.wq2, 1)
+
+    zbank = [[0, 1, 2, 3], [4, 5, 6, 7], [1, 2, 3, 4]]
+    ybank = [0, 5, 6]
+    land = [0] * NCH
+    for p, j, s, m in where:
+        if j == rank:
+            continue
+        call, src = [], cores[j]
+        for k, calls in enumerate(HELP[j]):
+            for q in calls:
+                if (rank, s, m) in q:
+                    call, src = q, helpers(j)[k]
+        if not call:
+            call = [q for q in DIRECT[j] if rank in q][0]
+        land[P["chunk_of"](rank, p, m)] += 2 * (len(bits(topo.mask(src, core))) // len(call))
+
+    def bank(k, m):
+        return T.ps[:, NC * k:NC * k + m]
+
+    def first_product(c):
+        a, b = chunks[c]
+        if land[c]:
+            te.wait_ge(T.sem["ch%d" % c], land[c])
+        for i in range(G):
+            if c == 2 and i == 3:
+                te.wait_ge(T.sem.vm, 5)
+            te.matmul_mx(bank(zbank[c][i], b - a), T.w1q[:, 128 * i:128 * i + 128], T.w1s[:, 128 * i:128 * i + 128],
+                         T.bc[:, EDGE + a:EDGE + b], T.bs[:, EDGE + a:EDGE + b], True, True).then_inc(T.sem.mm, 1)
+
+    def second_product(c):
+        a, b = chunks[c]
+        te.wait_ge(T.sem.hqd, c + 1)
+        te.matmul_mx(bank(ybank[c], b - a), T.w2q[:], T.w2s[:], T.hq[:, a:b], T.hs[:, a:b], True, True).then_inc(T.sem.my, 1)
+
+    te.wait_ge(T.sem.wq1, 1)
+    if own:
+        te.wait_ge(T.sem.own, 1)
+    first_product(0)
+    first_product(1)
+    te.wait_ge(T.sem.wq2, 1)
+    second_product(0)
+    first_product(2)
+    second_product(1)
+    second_product(2)
+
+    for c in range(NCH):
+        a, b = chunks[c]
+        v.wait_ge(T.sem["gbd%d" % c], 1)
+        for i in range(G):
+            v.wait_ge(T.sem.mm, G * c + i + 1)
+            v.tensor_tensor(T.hb[:, 4 * a + i:4 * b:4], bank(zbank[c][i], b - a), T.gb[:, a:b],
+                            AluOpType.mult).then_inc(T.sem.vm, 1)
+        v.wait_ge(T.sem.vm, G * c + G)
+        v.tensor_scalar(T.hb[:, 4 * a + 3:4 * b:4], T.hb[:, 4 * a + 3:4 * b:4], 0.0, C,
+                        AluOpType.max, AluOpType.mult).then_inc(T.sem.vr, 1)
+        v.wait_ge(T.sem.vr, c + 1)
+        v.wait_ge(T.sem.sr, 3 * (c + 1))
+        v.quantize_mx(T.hq[:, a:b], T.hs[:, a:b], T.hb[:, 4 * a:4 * b]).then_inc(T.sem.hqd, 1)
+
+    def relu(c):
+        a, b = chunks[c]
+        for i in range(G - 1):
+            sc.wait_ge(T.sem.vm, G * c + i + 1)
+            sc.activation(T.hb[:, 4 * a + i:4 * b:4], T.hb[:, 4 * a + i:4 * b:4], ActivationFunctionType.Relu,
+                          scale=C).then_inc(T.sem.sr, 1)
+
+    def y_out(c):
+        a, b = chunks[c]
+        sc.wait_ge(T.sem.my, c + 1)
+        sc.activation(T.ysb[:, a:b], bank(ybank[c], b - a), ActivationFunctionType.Copy).then_inc(T.sem["yc%d" % c], 1)
+
+    relu(0)
+    relu(1)
+    y_out(0)
+    relu(2)
+    y_out(1)
+    y_out(2)
+
+    stores = 0
+    for c in range(NCH):
+        a, b = chunks[c]
+        segs = []
+        for p, j, s, m in where:
+            lo, hi = max(p, a), min(p + m, b)
+            if lo < hi:
+                y0 = P["base"][rank][j] + s + lo - p
+                if segs and segs[-1][0] + segs[-1][2] == lo and segs[-1][1] + segs[-1][2] == y0:
+                    segs[-1] = (segs[-1][0], segs[-1][1], segs[-1][2] + hi - lo)
+                else:
+                    segs.append((lo, y0, hi - lo))
+        sy.wait_ge(T.sem["yc%d" % c], 1)
+        for lo, y0, m in segs:
+            sy.dma_start(T.y[:, y0:y0 + m], T.ysb[:, lo:lo + m]).then_inc(T.sem.yst, 16)
+            stores += 1
+    sy.wait_ge(T.sem.yst, 16 * stores)

@@ -4,20 +4,27 @@ from concourse.mybir import dt, AluOpType, ActivationFunctionType
 NC, G, EDGE, NCH = 512, 4, 128, 3
 CORES_SIMULATED = 256
 C = 2.0 ** -5
+XCUT = 384
+WCUT = 2
+AIM = (176, 368)
+ONSCALAR = (4, 4, 3)
 
 HELP = [
-    [[[(6, 0, 96)]], [[(2, 0, 48)]], [[(3, 0, 96)]], [[(3, 96, 96)]]],
-    [[[(0, 0, 96)]], [[(4, 0, 96)]], [[(5, 0, 128)]], [[(5, 128, 48), (7, 0, 48)], [(9, 0, 16)]]],
-    [[[(1, 0, 80)]], [[(8, 0, 16)]], [[(6, 0, 112)]], [[(4, 0, 96)]]],
-    [[[(5, 0, 80)]], [[(9, 0, 16)]], [[(2, 0, 96)]], [[(7, 0, 80)]]],
-    [[[(3, 0, 80)]], [[(8, 0, 16)]], [[(1, 0, 128)]], [[(0, 0, 96)]]],
-    [[[(1, 0, 80)]], [[(3, 0, 32)]], [[(4, 0, 64)]], [[(4, 64, 48)]]],
-    [[[(4, 0, 32)], [(5, 0, 16)]], [[(9, 0, 48)], [(7, 0, 16)]], [[(2, 0, 96)], [(0, 0, 16)]], [[(9, 48, 112)]]],
-    [[[(3, 0, 96)]], [[(0, 0, 80)]], [[(9, 0, 48)], [(6, 0, 16)]], [[(0, 80, 80)]]],
-    [[[(0, 0, 96)]], [[(2, 0, 80)]], [[(7, 0, 96)]], [[(2, 80, 80)], [(3, 0, 16)]]],
-    [[[(8, 144, 128)]], [[(8, 272, 128)]], [[(1, 0, 48)]], [[(8, 0, 144)]]],
+    [[[(3, 80, 112)]], [[(4, 0, 80)]], [[(6, 0, 96)]], [[(3, 0, 80)], [(2, 0, 48)]]],
+    [[[(7, 0, 48)], [(9, 0, 16)]], [[(0, 0, 96)]], [[(5, 32, 144)]], [[(4, 0, 96)], [(5, 0, 32)]]],
+    [[[(6, 32, 80)], [(8, 0, 16)]], [[(1, 0, 80)], [(0, 0, 32)]], [[(6, 0, 32)]], [[(4, 0, 96)]]],
+    [[[(8, 0, 64)], [(9, 0, 16)]], [[(5, 0, 80)]], [[(2, 0, 96)]], [[(7, 0, 80)]]],
+    [[[(8, 0, 16)]], [[(3, 0, 80)], [(5, 0, 16)]], [[(1, 16, 112)]], [[(0, 0, 96)], [(1, 0, 16)]]],
+    [[[(3, 0, 32)]], [[(2, 0, 96)]], [[(1, 0, 80)]], [[(9, 0, 96)]]],
+    [[[(3, 0, 96)]], [[(4, 0, 32)], [(5, 0, 16), (7, 0, 16)]], [[(2, 0, 96)], [(0, 0, 16)]], [[(9, 0, 160)]]],
+    [[[(5, 0, 80)], [(6, 0, 16)]], [[(0, 0, 96)]], [[(3, 0, 80)], [(2, 0, 16)]], [[(4, 0, 80)], [(3, 80, 16)]]],
+    [[[(1, 0, 48)]], [[(2, 0, 160)], [(3, 0, 16)]], [[(0, 0, 96)]], [[(7, 0, 96)], [(6, 0, 32)]]],
+    [[[(8, 0, 128)]], [[(8, 272, 128)]], [[(8, 128, 144)]], [[(1, 0, 48)], [(7, 0, 16)]]],
 ]
-DIRECT = [[[4, 7]], [], [[9], [0]], [[6], [8]], [[7], [5]], [[2, 9]], [[3]], [[4, 5], [2]], [[1], [6]], [[5], [7]]]
+DIRECT = [
+    [[(7, 0, 80)]], [], [[(9, 0, 176)]], [[(6, 0, 176)]], [[(7, 0, 160)]],
+    [[(4, 0, 112)]], [], [[(0, 96, 64)], [(9, 0, 48)]], [[(1, 48, 48)]], [[(5, 0, 48)]],
+]
 
 SCRATCH = {
     "xb": ("sbuf", [128, 4 * NC], "bfloat16"),
@@ -43,7 +50,7 @@ SCRATCH = {
     "ysb": ("sbuf", [128, NC], "float32"),
     "ps": ("psum", [128, 8 * NC], "float32"),
 }
-SEMAPHORES = (["gtl", "xl0", "xl1", "wl1", "wl2", "xqd", "own", "wq1", "wq2", "go", "ls", "hgs", "hcs", "hps",
+SEMAPHORES = (["gtl", "xl0", "xl1", "wl0", "wl1", "wl2", "xqd", "own", "wq1", "wq2", "go", "ls", "hgs", "hcs", "hps",
                "mm", "my", "vm", "vr", "sr", "hqd", "yst"]
               + ["g%d" % j for j in range(10)] + ["ch%d" % c for c in range(NCH)]
               + ["gth%d" % c for c in range(NCH)] + ["gbd%d" % c for c in range(NCH)] + ["yc%d" % c for c in range(NCH)])
@@ -65,32 +72,39 @@ def make_plan(tables):
     for j in range(n):
         if cnt[j][j]:
             pieces[j].append((-1, j, 0, cnt[j][j]))
+        for i, call in enumerate(DIRECT[j]):
+            for e, s, m in call:
+                pieces[e].append((i, j, s, m))
+                first.setdefault((j, e), -1)
         for k, calls in enumerate(HELP[j]):
             for i, call in enumerate(calls):
                 for e, s, m in call:
                     pieces[e].append((10 + i, j, s, m))
                     first.setdefault((j, e), k)
-        for i, call in enumerate(DIRECT[j]):
-            for e in call:
-                pieces[e].append((i, j, 0, cnt[j][e]))
-                first[(j, e)] = -1
-    place, chunks, turned = {}, [], []
+    place, chunks = {}, []
+    turned = []
     for e in range(n):
-        pieces[e].sort()
+        order = sorted(pieces[e])
         turn = bool(cnt[e][e]) and off[e][e + 1] < 128
         turned.append(turn)
-        at, ends = 0, []
-        for _, j, s, m in pieces[e]:
-            place[(e, j, s)] = NC - at - m if turn else at
-            at += m
-            ends.append(at)
+        ends = [sum(p[3] for p in order[:k + 1]) for k in range(len(order))]
         best = None
         for a in range(128, 257, 16):
             for b in range(a + 128, NC - 127, 16):
-                v = abs(a - 240) / 16 + abs(b - 384) / 16 + (0 if a in ends else 3) + (0 if b in ends else 3)
+                v = abs(a - AIM[0]) / 16 + abs(b - AIM[1]) / 16 + (0 if a in ends else 3) + (0 if b in ends else 3)
                 if best is None or v < best[0]:
                     best = (v, a, b)
         cut = [0, best[1], best[2], NC]
+        for c in range(NCH):
+            inside = [k for k, p in enumerate(order)
+                      if p[0] >= 0 and ends[k] - p[3] >= cut[c] and ends[k] <= cut[c + 1]]
+            if inside:
+                lo, hi = inside[0], inside[-1] + 1
+                order[lo:hi] = sorted(order[lo:hi], key=lambda p: p[1:3], reverse=turn)
+        at = 0
+        for _, j, s, m in order:
+            place[(e, j, s)] = NC - at - m if turn else at
+            at += m
         chunks.append([(NC - cut[c + 1], NC - cut[c]) if turn else (cut[c], cut[c + 1]) for c in range(NCH)])
     base = [[sum(cnt[i][e] for i in range(j)) for j in range(n)] for e in range(n)]
 
@@ -130,6 +144,15 @@ def rank_program(g, core, T, topo):
         return
     P = make_plan(T.tables)
     sent = [0]
+
+    def straight(j):
+        return [cores[e] for e in sorted({e for call in DIRECT[j] for e, s, m in call})]
+
+    def gate_mask(j):
+        near = topo.mask(cores[j], helpers(j)[0])
+        for d in straight(j):
+            near &= ~topo.mask(cores[j], d)
+        return near
 
     def dst(d):
         rid, pid = topo.addr(d, core)
@@ -174,7 +197,7 @@ def rank_program(g, core, T, topo):
         starts = windows(P, j)[1]
         here = len(bits(topo.mask(cores[j], core)))
         to = sorted(e for (src, e), by in P["first"].items() if src == j and by == k)
-        g.wait_ge(T.sem.hgs, here)
+        g.wait_ge(T.sem.hgs, len(bits(gate_mask(j))))
         if to:
             send_gates([(cores[e], T.gl[j]) for e in to], T.sem["g%d" % j], topo.mask(core, cores[to[0]]))
         for call in HELP[j][k]:
@@ -190,10 +213,16 @@ def rank_program(g, core, T, topo):
     own = cnt[rank][rank]
     where = sorted((P["place"][(rank, j, s)], j, s, m) for _, j, s, m in P["pieces"][rank])
     sy, sc, v, te = g.sync, g.scalar, g.vector, g.tensor
+    wc = 128 * WCUT
 
-    sy.dma_start(T.gd[:], T.gt[0:1, :]).then_inc(T.sem.gtl, 16)
-    sc.dma_start(T.xb[:, 0:2 * NC], T.x[:, 0:2 * NC]).then_inc(T.sem.xl0, 16)
-    sy.dma_start(T.xb[:, 2 * NC:4 * NC], T.x[:, 2 * NC:4 * NC]).then_inc(T.sem.xl1, 16)
+    sc.dma_start(T.gd[:], T.gt[0:1, :]).then_inc(T.sem.gtl, 16)
+    sc.dma_start(T.xb[:, 0:4 * XCUT], T.x[:, 0:4 * XCUT]).then_inc(T.sem.xl0, 16)
+    sc.dma_start(T.xb[:, 4 * XCUT:4 * NC], T.x[:, 4 * XCUT:4 * NC]).then_inc(T.sem.xl1, 16)
+    sc.dma_start(T.w1b[:, 0:4 * wc], T.w1[:, 0:4 * wc]).then_inc(T.sem.wl0, 16)
+    sc.wait_ge(T.sem.go, 1)
+    if WCUT < 4:
+        sc.dma_start(T.w1b[:, 4 * wc:4 * NC], T.w1[:, 4 * wc:4 * NC]).then_inc(T.sem.wl1, 16)
+    sc.dma_start(T.w2b[:], T.w2[:]).then_inc(T.sem.wl2, 16)
 
     runs = [[] for _ in range(NCH)]
     for p, j, s, m in where:
@@ -207,11 +236,6 @@ def rank_program(g, core, T, topo):
         for p, j, t0, m in runs[c]:
             if j == rank:
                 sy.dma_start(T.grow[0:1, p:p + m], T.gt[0:1, t0:t0 + m]).then_inc(T.sem["gth%d" % c], 16)
-
-    sy.wait_ge(T.sem.go, 1)
-    sy.dma_start(T.w1b[:], T.w1[:]).then_inc(T.sem.wl1, 16)
-    sy.dma_start(T.w2b[:], T.w2[:]).then_inc(T.sem.wl2, 16)
-
     seen = set()
     for c in range(NCH):
         todo = [r for r in runs[c] if r[1] != rank]
@@ -226,10 +250,9 @@ def rank_program(g, core, T, topo):
 
     near = topo.mask(core, hs[0])
     g.wait_ge(T.sem.gtl, 16)
-    send_gates([(h, T.gd[:]) for h in hs], T.sem.hgs, near)
-    straight = [cores[e] for call in DIRECT[rank] for e in call]
-    if straight:
-        send_gates([(d, T.gl[rank]) for d in straight], T.sem["g%d" % rank], topo.mask(core, straight[0]))
+    send_gates([(h, T.gd[:]) for h in hs], T.sem.hgs, gate_mask(rank))
+    if straight(rank):
+        send_gates([(d, T.gl[rank]) for d in straight(rank)], T.sem["g%d" % rank], topo.mask(core, straight(rank)[0]))
     g.wait_ge(T.sem.xqd, 2)
     turn = [0, 2, 1, 3]
     send([(codes(T.xq, a, a + width), h, codes(T.hc, 0, width), T.sem.hcs, share(near, turn[k], 4))
@@ -238,7 +261,7 @@ def rank_program(g, core, T, topo):
           for k, (h, a) in enumerate(zip(hs, starts))])
     g.sem_inc(T.sem.go, 1)
     for call in DIRECT[rank]:
-        pass_on(rank, [(e, 0, cnt[rank][e]) for e in call], T.xq, T.xs, 0, lambda kind: None)
+        pass_on(rank, call, T.xq, T.xs, 0, lambda kind: None)
     for c in range(NCH):
         a, b = chunks[c]
         if runs[c]:
@@ -247,17 +270,20 @@ def rank_program(g, core, T, topo):
     g.wait_ge(T.sem.ls, sent[0])
 
     v.wait_ge(T.sem.xl0, 16)
-    v.quantize_mx(T.xq[:, 0:NC // 2], T.xs[:, 0:NC // 2], T.xb[:, 0:2 * NC]).then_inc(T.sem.xqd, 1)
+    v.quantize_mx(T.xq[:, 0:XCUT], T.xs[:, 0:XCUT], T.xb[:, 0:4 * XCUT]).then_inc(T.sem.xqd, 1)
     v.wait_ge(T.sem.xl1, 16)
-    v.quantize_mx(T.xq[:, NC // 2:NC], T.xs[:, NC // 2:NC], T.xb[:, 2 * NC:4 * NC]).then_inc(T.sem.xqd, 1)
+    v.quantize_mx(T.xq[:, XCUT:NC], T.xs[:, XCUT:NC], T.xb[:, 4 * XCUT:4 * NC]).then_inc(T.sem.xqd, 1)
     if own:
         if P["turned"][rank]:
             xa, ba = off[rank][rank], EDGE + NC - own
         else:
             xa, ba = off[rank][rank + 1] - 128, EDGE + own - 128
         v.quantize_mx(T.bc[:, ba:ba + 128], T.bs[:, ba:ba + 128], T.xb[:, 4 * xa:4 * (xa + 128)]).then_inc(T.sem.own, 1)
-    v.wait_ge(T.sem.wl1, 16)
-    v.quantize_mx(T.w1q[:], T.w1s[:], T.w1b[:]).then_inc(T.sem.wq1, 1)
+    v.wait_ge(T.sem.wl0, 16)
+    v.quantize_mx(T.w1q[:, 0:wc], T.w1s[:, 0:wc], T.w1b[:, 0:4 * wc]).then_inc(T.sem.wq1, 1)
+    if WCUT < 4:
+        v.wait_ge(T.sem.wl1, 16)
+        v.quantize_mx(T.w1q[:, wc:NC], T.w1s[:, wc:NC], T.w1b[:, 4 * wc:4 * NC]).then_inc(T.sem.wq1, 1)
     v.wait_ge(T.sem.wl2, 16)
     v.quantize_mx(T.w2q[:], T.w2s[:], T.w2b[:]).then_inc(T.sem.wq2, 1)
 
@@ -273,7 +299,7 @@ def rank_program(g, core, T, topo):
                 if (rank, s, m) in q:
                     call, src = q, helpers(j)[k]
         if not call:
-            call = [q for q in DIRECT[j] if rank in q][0]
+            call = [q for q in DIRECT[j] if (rank, s, m) in q][0]
         land[P["chunk_of"](rank, p, m)] += 2 * (len(bits(topo.mask(src, core))) // len(call))
 
     def bank(k, m):
@@ -294,7 +320,7 @@ def rank_program(g, core, T, topo):
         te.wait_ge(T.sem.hqd, c + 1)
         te.matmul_mx(bank(ybank[c], b - a), T.w2q[:], T.w2s[:], T.hq[:, a:b], T.hs[:, a:b], True, True).then_inc(T.sem.my, 1)
 
-    te.wait_ge(T.sem.wq1, 1)
+    te.wait_ge(T.sem.wq1, 2 if WCUT < 4 else 1)
     if own:
         te.wait_ge(T.sem.own, 1)
     first_product(0)
@@ -305,23 +331,43 @@ def rank_program(g, core, T, topo):
     second_product(1)
     second_product(2)
 
-    for c in range(NCH):
+    relus = [sum(ONSCALAR[:c + 1]) for c in range(NCH)]
+    left = [sum(G - k for k in ONSCALAR[:c + 1]) for c in range(NCH)]
+
+    def times_gate(c, i):
         a, b = chunks[c]
-        v.wait_ge(T.sem["gbd%d" % c], 1)
-        for i in range(G):
-            v.wait_ge(T.sem.mm, G * c + i + 1)
-            v.tensor_tensor(T.hb[:, 4 * a + i:4 * b:4], bank(zbank[c][i], b - a), T.gb[:, a:b],
-                            AluOpType.mult).then_inc(T.sem.vm, 1)
-        v.wait_ge(T.sem.vm, G * c + G)
-        v.tensor_scalar(T.hb[:, 4 * a + 3:4 * b:4], T.hb[:, 4 * a + 3:4 * b:4], 0.0, C,
-                        AluOpType.max, AluOpType.mult).then_inc(T.sem.vr, 1)
-        v.wait_ge(T.sem.vr, c + 1)
-        v.wait_ge(T.sem.sr, 3 * (c + 1))
+        if i == 0:
+            v.wait_ge(T.sem["gbd%d" % c], 1)
+        v.wait_ge(T.sem.mm, G * c + i + 1)
+        v.tensor_tensor(T.hb[:, 4 * a + i:4 * b:4], bank(zbank[c][i], b - a), T.gb[:, a:b],
+                        AluOpType.mult).then_inc(T.sem.vm, 1)
+
+    def last_relu(c):
+        a, b = chunks[c]
+        for i in range(ONSCALAR[c], G):
+            v.wait_ge(T.sem.vm, G * c + i + 1)
+            v.tensor_scalar(T.hb[:, 4 * a + i:4 * b:4], T.hb[:, 4 * a + i:4 * b:4], 0.0, C,
+                            AluOpType.max, AluOpType.mult).then_inc(T.sem.vr, 1)
+
+    def pack(c):
+        a, b = chunks[c]
+        if left[c]:
+            v.wait_ge(T.sem.vr, left[c])
+        v.wait_ge(T.sem.sr, relus[c])
         v.quantize_mx(T.hq[:, a:b], T.hs[:, a:b], T.hb[:, 4 * a:4 * b]).then_inc(T.sem.hqd, 1)
+
+    for c in range(NCH):
+        for i in range(0 if c == 0 else 2, G):
+            times_gate(c, i)
+        if c + 1 < NCH:
+            times_gate(c + 1, 0)
+            times_gate(c + 1, 1)
+        last_relu(c)
+        pack(c)
 
     def relu(c):
         a, b = chunks[c]
-        for i in range(G - 1):
+        for i in range(ONSCALAR[c]):
             sc.wait_ge(T.sem.vm, G * c + i + 1)
             sc.activation(T.hb[:, 4 * a + i:4 * b:4], T.hb[:, 4 * a + i:4 * b:4], ActivationFunctionType.Relu,
                           scale=C).then_inc(T.sem.sr, 1)

from concourse.bass import DstId, RemoteDMATransfer
from concourse.mybir import dt, AluOpType, ActivationFunctionType

NC, G, EDGE, NCH = 512, 4, 128, 3
CORES_SIMULATED = 256
C = 2.0 ** -5
XCUT = 384
WCUT = 2
AIM = (176, 368)
ONSCALAR = (4, 4, 3)

HELP = [
    [[[(3, 80, 112)]], [[(4, 0, 80)]], [[(6, 0, 96)]], [[(3, 0, 80)], [(2, 0, 48)]]],
    [[[(7, 0, 48)], [(9, 0, 16)]], [[(0, 0, 96)]], [[(5, 32, 144)]], [[(4, 0, 96)], [(5, 0, 32)]]],
    [[[(6, 32, 80)], [(8, 0, 16)]], [[(1, 0, 80)], [(0, 0, 32)]], [[(6, 0, 32)]], [[(4, 0, 96)]]],
    [[[(8, 0, 64)], [(9, 0, 16)]], [[(5, 0, 80)]], [[(2, 0, 96)]], [[(7, 0, 80)]]],
    [[[(8, 0, 16)]], [[(3, 0, 80)], [(5, 0, 16)]], [[(1, 16, 112)]], [[(0, 0, 96)], [(1, 0, 16)]]],
    [[[(3, 0, 32)]], [[(2, 0, 96)]], [[(1, 0, 80)]], [[(9, 0, 96)]]],
    [[[(3, 0, 96)]], [[(4, 0, 32)], [(5, 0, 16), (7, 0, 16)]], [[(2, 0, 96)], [(0, 0, 16)]], [[(9, 0, 160)]]],
    [[[(5, 0, 80)], [(6, 0, 16)]], [[(0, 0, 96)]], [[(3, 0, 80)], [(2, 0, 16)]], [[(4, 0, 80)], [(3, 80, 16)]]],
    [[[(1, 0, 48)]], [[(2, 0, 160)], [(3, 0, 16)]], [[(0, 0, 96)]], [[(7, 0, 96)], [(6, 0, 32)]]],
    [[[(8, 0, 128)]], [[(8, 272, 128)]], [[(8, 128, 144)]], [[(1, 0, 48)], [(7, 0, 16)]]],
]
DIRECT = [
    [[(7, 0, 80)]], [], [[(9, 0, 176)]], [[(6, 0, 176)]], [[(7, 0, 160)]],
    [[(4, 0, 112)]], [], [[(0, 96, 64)], [(9, 0, 48)]], [[(1, 48, 48)]], [[(5, 0, 48)]],
]

SCRATCH = {
    "xb": ("sbuf", [128, 4 * NC], "bfloat16"),
    "w1b": ("sbuf", [128, 4 * NC], "bfloat16"),
    "w2b": ("sbuf", [128, NC], "bfloat16"),
    "xq": ("sbuf", [128, NC], "float8_e4m3fn_x4"),
    "xs": ("sbuf", [128, NC], "uint8"),
    "w1q": ("sbuf", [128, NC], "float8_e4m3fn_x4"),
    "w1s": ("sbuf", [128, NC], "uint8"),
    "w2q": ("sbuf", [128, 128], "float8_e4m3fn_x4"),
    "w2s": ("sbuf", [128, 128], "uint8"),
    "hc": ("sbuf", [128, 192], "float8_e4m3fn_x4"),
    "hp": ("sbuf", [128, 192], "uint8"),
    "bc": ("sbuf", [128, NC + 2 * EDGE], "float8_e4m3fn_x4"),
    "bs": ("sbuf", [128, NC + 2 * EDGE], "uint8"),
    "gd": ("dram", [128, 4], "bfloat16"),
    "gl": ("dram", [10, 128, 4], "bfloat16"),
    "grow": ("sbuf", [128, NC], "bfloat16"),
    "gb": ("sbuf", [128, NC], "bfloat16"),
    "hb": ("sbuf", [128, 4 * NC], "bfloat16"),
    "hq": ("sbuf", [128, NC], "float8_e4m3fn_x4"),
    "hs": ("sbuf", [128, NC], "uint8"),
    "ysb": ("sbuf", [128, NC], "float32"),
    "ps": ("psum", [128, 8 * NC], "float32"),
}
SEMAPHORES = (["gtl", "xl0", "xl1", "wl0", "wl1", "wl2", "xqd", "own", "wq1", "wq2", "go", "ls", "hgs", "hcs", "hps",
               "mm", "my", "vm", "vr", "sr", "hqd", "yst"]
              + ["g%d" % j for j in range(10)] + ["ch%d" % c for c in range(NCH)]
              + ["gth%d" % c for c in range(NCH)] + ["gbd%d" % c for c in range(NCH)] + ["yc%d" % c for c in range(NCH)])


def bits(mask):
    return [b for b in range(mask.bit_length()) if mask >> b & 1]


def share(mask, k, n):
    return sum(1 << b for b in bits(mask)[k::n])


def make_plan(tables):
    cnt, n = tables["CNT"], len(tables["CNT"])
    off = [[sum(row[:e]) for e in range(n + 1)] for row in cnt]
    pieces = [[] for _ in range(n)]
    first = {}
    for j in range(n):
        if cnt[j][j]:
            pieces[j].append((-1, j, 0, cnt[j][j]))
        for i, call in enumerate(DIRECT[j]):
            for e, s, m in call:
                pieces[e].append((i, j, s, m))
                first.setdefault((j, e), -1)
        for k, calls in enumerate(HELP[j]):
            for i, call in enumerate(calls):
                for e, s, m in call:
                    pieces[e].append((10 + i, j, s, m))
                    first.setdefault((j, e), k)
    place, chunks = {}, []
    turned = []
    for e in range(n):
        order = sorted(pieces[e])
        turn = bool(cnt[e][e]) and off[e][e + 1] < 128
        turned.append(turn)
        ends = [sum(p[3] for p in order[:k + 1]) for k in range(len(order))]
        best = None
        for a in range(128, 257, 16):
            for b in range(a + 128, NC - 127, 16):
                v = abs(a - AIM[0]) / 16 + abs(b - AIM[1]) / 16 + (0 if a in ends else 3) + (0 if b in ends else 3)
                if best is None or v < best[0]:
                    best = (v, a, b)
        cut = [0, best[1], best[2], NC]
        for c in range(NCH):
            inside = [k for k, p in enumerate(order)
                      if p[0] >= 0 and ends[k] - p[3] >= cut[c] and ends[k] <= cut[c + 1]]
            if inside:
                lo, hi = inside[0], inside[-1] + 1
                order[lo:hi] = sorted(order[lo:hi], key=lambda p: p[1:3], reverse=turn)
        at = 0
        for _, j, s, m in order:
            place[(e, j, s)] = NC - at - m if turn else at
            at += m
        chunks.append([(NC - cut[c + 1], NC - cut[c]) if turn else (cut[c], cut[c + 1]) for c in range(NCH)])
    base = [[sum(cnt[i][e] for i in range(j)) for j in range(n)] for e in range(n)]

    def chunk_of(e, p, m):
        return min(c for c in range(NCH) if p < chunks[e][c][1] and p + m > chunks[e][c][0])
    return {"cnt": cnt, "off": off, "pieces": pieces, "first": first, "place": place, "chunks": chunks,
            "turned": turned, "base": base, "chunk_of": chunk_of}


def windows(P, j):
    spans = []
    for calls in HELP[j]:
        cols = [(P["off"][j][e] + s, P["off"][j][e] + s + m) for call in calls for e, s, m in call]
        spans.append((min(a for a, _ in cols), max(b for _, b in cols)))
    w = max(b - a for a, b in spans)
    return w, [min(a, NC - w) for a, _ in spans]


def rank_program(g, core, T, topo):
    cores = T.cores
    rank = T.rank_of(core)
    known = {}

    def same_chip(a, b):
        return topo.chip(a) == topo.chip(b) and topo.host(a) == topo.host(b)

    def helpers(j):
        if j not in known:
            r = cores[j]
            own = [c for c in range(CORES_SIMULATED)
                   if c != r and same_chip(c, r) and all(topo.may_write(c, d) for d in cores)]
            known[j] = sorted(own, key=lambda c: (topo.die(c) != topo.die(r), c))
        return known[j]

    serves = [j for j in range(len(cores)) if same_chip(core, cores[j]) and (rank is not None or core in helpers(j))]
    if not serves:
        return
    P = make_plan(T.tables)
    sent = [0]

    def straight(j):
        return [cores[e] for e in sorted({e for call in DIRECT[j] for e, s, m in call})]

    def gate_mask(j):
        near = topo.mask(cores[j], helpers(j)[0])
        for d in straight(j):
            near &= ~topo.mask(cores[j], d)
        return near

    def dst(d):
        rid, pid = topo.addr(d, core)
        return DstId(rid=rid, pnc=pid)

    def send(parts):
        sent[0] += sum(len(bits(p[4])) for p in parts)
        if len(parts) == 1:
            src, d, out, sem, mask = parts[0]
            rid, pid = topo.addr(d, core)
            g.remote_dma(out, src, sem, T.sem.ls, pid, rid, mask)
        else:
            g.remote_dma_fused([RemoteDMATransfer(dst_ids=[dst(d)], dma_engine_mask=mask, remote_sem=sem, src=src, dst=out)
                                for src, d, out, sem, mask in parts], local_sem=T.sem.ls)

    def send_gates(outs, sem, mask):
        sent[0] += len(bits(mask))
        g.remote_dma_fused([RemoteDMATransfer(dst_ids=[dst(d) for d, _ in outs], dma_engine_mask=mask, remote_sem=sem,
                                              srcs=[T.gd[:]], dsts=[o for _, o in outs])], local_sem=T.sem.ls)

    def codes(t, a, b):
        return t[:, a:b].bitcast(dt.uint8)

    def pass_on(j, call, qc, qs, first_col, before):
        for kind in range(2):
            before(kind)
            parts = []
            for i, (e, s, m) in enumerate(call):
                a = P["off"][j][e] + s - first_col
                p = P["place"][(e, j, s)]
                sem = T.sem["ch%d" % P["chunk_of"](e, p, m)]
                mask = share(topo.mask(core, cores[e]), i, len(call))
                if kind == 0:
                    parts.append((codes(qc, a, a + m), cores[e], codes(T.bc, EDGE + p, EDGE + p + m), sem, mask))
                else:
                    parts.append((qs[:, a:a + m], cores[e], T.bs[:, EDGE + p:EDGE + p + m], sem, mask))
            send(parts)

    if rank is None:
        j = serves[0]
        k = helpers(j).index(core)
        starts = windows(P, j)[1]
        here = len(bits(topo.mask(cores[j], core)))
        to = sorted(e for (src, e), by in P["first"].items() if src == j and by == k)
        g.wait_ge(T.sem.hgs, len(bits(gate_mask(j))))
        if to:
            send_gates([(cores[e], T.gl[j]) for e in to], T.sem["g%d" % j], topo.mask(core, cores[to[0]]))
        for call in HELP[j][k]:
            pass_on(j, call, T.hc, T.hp, starts[k],
                    lambda kind: g.wait_ge([T.sem.hcs, T.sem.hps][kind], here // 4))
        g.wait_ge(T.sem.ls, sent[0])
        return

    cnt, off = P["cnt"], P["off"]
    hs = helpers(rank)
    width, starts = windows(P, rank)
    chunks = P["chunks"][rank]
    own = cnt[rank][rank]
    where = sorted((P["place"][(rank, j, s)], j, s, m) for _, j, s, m in P["pieces"][rank])
    sy, sc, v, te = g.sync, g.scalar, g.vector, g.tensor
    wc = 128 * WCUT

    sc.dma_start(T.gd[:], T.gt[0:1, :]).then_inc(T.sem.gtl, 16)
    sc.dma_start(T.xb[:, 0:4 * XCUT], T.x[:, 0:4 * XCUT]).then_inc(T.sem.xl0, 16)
    sc.dma_start(T.xb[:, 4 * XCUT:4 * NC], T.x[:, 4 * XCUT:4 * NC]).then_inc(T.sem.xl1, 16)
    sc.dma_start(T.w1b[:, 0:4 * wc], T.w1[:, 0:4 * wc]).then_inc(T.sem.wl0, 16)
    sc.wait_ge(T.sem.go, 1)
    if WCUT < 4:
        sc.dma_start(T.w1b[:, 4 * wc:4 * NC], T.w1[:, 4 * wc:4 * NC]).then_inc(T.sem.wl1, 16)
    sc.dma_start(T.w2b[:], T.w2[:]).then_inc(T.sem.wl2, 16)

    runs = [[] for _ in range(NCH)]
    for p, j, s, m in where:
        r = runs[P["chunk_of"](rank, p, m)]
        t0 = off[j][rank] + s
        if r and r[-1][1] == j and r[-1][0] + r[-1][3] == p and r[-1][2] + r[-1][3] == t0:
            r[-1] = (r[-1][0], j, r[-1][2], r[-1][3] + m)
        else:
            r.append((p, j, t0, m))
    for c in range(NCH):
        for p, j, t0, m in runs[c]:
            if j == rank:
                sy.dma_start(T.grow[0:1, p:p + m], T.gt[0:1, t0:t0 + m]).then_inc(T.sem["gth%d" % c], 16)
    seen = set()
    for c in range(NCH):
        todo = [r for r in runs[c] if r[1] != rank]
        todo.sort(key=lambda r: (P["first"][(r[1], rank)] >= 0, r[1]))
        for p, j, t0, m in todo:
            if j not in seen:
                seen.add(j)
                sender = P["first"][(j, rank)]
                src = cores[j] if sender < 0 else helpers(j)[sender]
                sy.wait_ge(T.sem["g%d" % j], len(bits(topo.mask(src, core))))
            sy.dma_start(T.grow[0:1, p:p + m], T.gl[j, t0 // 4:(t0 + m) // 4, :]).then_inc(T.sem["gth%d" % c], 16)

    near = topo.mask(core, hs[0])
    g.wait_ge(T.sem.gtl, 16)
    send_gates([(h, T.gd[:]) for h in hs], T.sem.hgs, gate_mask(rank))
    if straight(rank):
        send_gates([(d, T.gl[rank]) for d in straight(rank)], T.sem["g%d" % rank], topo.mask(core, straight(rank)[0]))
    g.wait_ge(T.sem.xqd, 2)
    turn = [0, 2, 1, 3]
    send([(codes(T.xq, a, a + width), h, codes(T.hc, 0, width), T.sem.hcs, share(near, turn[k], 4))
          for k, (h, a) in enumerate(zip(hs, starts))])
    send([(T.xs[:, a:a + width], h, T.hp[:, 0:width], T.sem.hps, share(near, turn[k], 4))
          for k, (h, a) in enumerate(zip(hs, starts))])
    g.sem_inc(T.sem.go, 1)
    for call in DIRECT[rank]:
        pass_on(rank, call, T.xq, T.xs, 0, lambda kind: None)
    for c in range(NCH):
        a, b = chunks[c]
        if runs[c]:
            g.wait_ge(T.sem["gth%d" % c], 16 * len(runs[c]))
        g.partition_broadcast(T.gb[:, a:b], T.grow[0:1, a:b], 128).then_inc(T.sem["gbd%d" % c], 1)
    g.wait_ge(T.sem.ls, sent[0])

    v.wait_ge(T.sem.xl0, 16)
    v.quantize_mx(T.xq[:, 0:XCUT], T.xs[:, 0:XCUT], T.xb[:, 0:4 * XCUT]).then_inc(T.sem.xqd, 1)
    v.wait_ge(T.sem.xl1, 16)
    v.quantize_mx(T.xq[:, XCUT:NC], T.xs[:, XCUT:NC], T.xb[:, 4 * XCUT:4 * NC]).then_inc(T.sem.xqd, 1)
    if own:
        if P["turned"][rank]:
            xa, ba = off[rank][rank], EDGE + NC - own
        else:
            xa, ba = off[rank][rank + 1] - 128, EDGE + own - 128
        v.quantize_mx(T.bc[:, ba:ba + 128], T.bs[:, ba:ba + 128], T.xb[:, 4 * xa:4 * (xa + 128)]).then_inc(T.sem.own, 1)
    v.wait_ge(T.sem.wl0, 16)
    v.quantize_mx(T.w1q[:, 0:wc], T.w1s[:, 0:wc], T.w1b[:, 0:4 * wc]).then_inc(T.sem.wq1, 1)
    if WCUT < 4:
        v.wait_ge(T.sem.wl1, 16)
        v.quantize_mx(T.w1q[:, wc:NC], T.w1s[:, wc:NC], T.w1b[:, 4 * wc:4 * NC]).then_inc(T.sem.wq1, 1)
    v.wait_ge(T.sem.wl2, 16)
    v.quantize_mx(T.w2q[:], T.w2s[:], T.w2b[:]).then_inc(T.sem.wq2, 1)

    zbank = [[0, 1, 2, 3], [4, 5, 6, 7], [1, 2, 3, 4]]
    ybank = [0, 5, 6]
    land = [0] * NCH
    for p, j, s, m in where:
        if j == rank:
            continue
        call, src = [], cores[j]
        for k, calls in enumerate(HELP[j]):
            for q in calls:
                if (rank, s, m) in q:
                    call, src = q, helpers(j)[k]
        if not call:
            call = [q for q in DIRECT[j] if (rank, s, m) in q][0]
        land[P["chunk_of"](rank, p, m)] += 2 * (len(bits(topo.mask(src, core))) // len(call))

    def bank(k, m):
        return T.ps[:, NC * k:NC * k + m]

    def first_product(c):
        a, b = chunks[c]
        if land[c]:
            te.wait_ge(T.sem["ch%d" % c], land[c])
        for i in range(G):
            if c == 2 and i == 3:
                te.wait_ge(T.sem.vm, 5)
            te.matmul_mx(bank(zbank[c][i], b - a), T.w1q[:, 128 * i:128 * i + 128], T.w1s[:, 128 * i:128 * i + 128],
                         T.bc[:, EDGE + a:EDGE + b], T.bs[:, EDGE + a:EDGE + b], True, True).then_inc(T.sem.mm, 1)

    def second_product(c):
        a, b = chunks[c]
        te.wait_ge(T.sem.hqd, c + 1)
        te.matmul_mx(bank(ybank[c], b - a), T.w2q[:], T.w2s[:], T.hq[:, a:b], T.hs[:, a:b], True, True).then_inc(T.sem.my, 1)

    te.wait_ge(T.sem.wq1, 2 if WCUT < 4 else 1)
    if own:
        te.wait_ge(T.sem.own, 1)
    first_product(0)
    first_product(1)
    te.wait_ge(T.sem.wq2, 1)
    second_product(0)
    first_product(2)
    second_product(1)
    second_product(2)

    relus = [sum(ONSCALAR[:c + 1]) for c in range(NCH)]
    left = [sum(G - k for k in ONSCALAR[:c + 1]) for c in range(NCH)]

    def times_gate(c, i):
        a, b = chunks[c]
        if i == 0:
            v.wait_ge(T.sem["gbd%d" % c], 1)
        v.wait_ge(T.sem.mm, G * c + i + 1)
        v.tensor_tensor(T.hb[:, 4 * a + i:4 * b:4], bank(zbank[c][i], b - a), T.gb[:, a:b],
                        AluOpType.mult).then_inc(T.sem.vm, 1)

    def last_relu(c):
        a, b = chunks[c]
        for i in range(ONSCALAR[c], G):
            v.wait_ge(T.sem.vm, G * c + i + 1)
            v.tensor_scalar(T.hb[:, 4 * a + i:4 * b:4], T.hb[:, 4 * a + i:4 * b:4], 0.0, C,
                            AluOpType.max, AluOpType.mult).then_inc(T.sem.vr, 1)

    def pack(c):
        a, b = chunks[c]
        if left[c]:
            v.wait_ge(T.sem.vr, left[c])
        v.wait_ge(T.sem.sr, relus[c])
        v.quantize_mx(T.hq[:, a:b], T.hs[:, a:b], T.hb[:, 4 * a:4 * b]).then_inc(T.sem.hqd, 1)

    for c in range(NCH):
        for i in range(0 if c == 0 else 2, G):
            times_gate(c, i)
        if c + 1 < NCH:
            times_gate(c + 1, 0)
            times_gate(c + 1, 1)
        last_relu(c)
        pack(c)

    def relu(c):
        a, b = chunks[c]
        for i in range(ONSCALAR[c]):
            sc.wait_ge(T.sem.vm, G * c + i + 1)
            sc.activation(T.hb[:, 4 * a + i:4 * b:4], T.hb[:, 4 * a + i:4 * b:4], ActivationFunctionType.Relu,
                          scale=C).then_inc(T.sem.sr, 1)

    def y_out(c):
        a, b = chunks[c]
        sc.wait_ge(T.sem.my, c + 1)
        sc.activation(T.ysb[:, a:b], bank(ybank[c], b - a), ActivationFunctionType.Copy).then_inc(T.sem["yc%d" % c], 1)

    relu(0)
    relu(1)
    y_out(0)
    relu(2)
    y_out(1)
    y_out(2)

    stores = 0
    for c in range(NCH):
        a, b = chunks[c]
        segs = []
        for p, j, s, m in where:
            lo, hi = max(p, a), min(p + m, b)
            if lo < hi:
                y0 = P["base"][rank][j] + s + lo - p
                if segs and segs[-1][0] + segs[-1][2] == lo and segs[-1][1] + segs[-1][2] == y0:
                    segs[-1] = (segs[-1][0], segs[-1][1], segs[-1][2] + hi - lo)
                else:
                    segs.append((lo, y0, hi - lo))
        sy.wait_ge(T.sem["yc%d" % c], 1)
        for lo, y0, m in segs:
            sy.dma_start(T.y[:, y0:y0 + m], T.ysb[:, lo:lo + m]).then_inc(T.sem.yst, 16)
            stores += 1
    sy.wait_ge(T.sem.yst, 16 * stores)
